import numpy as np, ml_dtypes
CORES = [23,119,17,113]
N = 4
import mx_ref
NC, KT = 512, 2
FROM = [1,0,3,2]
BF = ml_dtypes.bfloat16
def setup_inputs(rng):
    def f(*shape):
        return mx_ref.flush((rng.standard_normal(shape, dtype=np.float32) * np.exp2(rng.integers(-2, 3, shape[:-1] + (1,)))).astype(BF))
    return {"w": f(N, 128, KT * 512), "x": f(N, 128, KT * 4 * NC)}
def setup_inputs_blocks(rng):
    d = setup_inputs(rng)
    for k in ("w", "x"): d[k] = mx_ref.spread(d[k], rng, 4)
    return d
def setup_inputs_wide(rng):
    d = setup_inputs(rng)
    for k in ("w", "x"): d[k] = mx_ref.flush((d[k].astype(np.float32) * np.exp2(rng.integers(-8, 9, (N, 1, 1))).astype(np.float32)).astype(BF))
    return d
def setup_inputs_zeros(rng):
    d = setup_inputs(rng); v = d["x"].reshape(N, 128, -1, 4).copy()
    v[np.broadcast_to((rng.random((N, 1, v.shape[2], 1)) < 0.33), v.shape)] = 0
    d["x"] = v.reshape(d["x"].shape)
    return d
def reference(w, x):
    y = np.zeros((N, 128, NC), np.float32)
    for r in range(N):
        for t in range(KT):
            p = mx_ref.matmul(mx_ref.quantize(w[r][:, 512 * t:512 * t + 512]), mx_ref.quantize(x[FROM[r]][:, 4 * NC * t:4 * NC * t + 4 * NC]))
            y[r] = p if t == 0 else y[r] + p
    return {"y": y}

from concourse.mybir import dt, ActivationFunctionType

KT, NC, WM = 2, 512, 128
TOTAL = KT * NC

PIECES = [(0, 128), (128, 512), (512, 1024)]
SENDS = [("codes", 0, 128), ("codes", 128, 512), ("scales", 0, 1024),
         ("codes", 512, 896), ("codes", 896, 1024)]
GROUPS = [(0, 384), (384, 512)]

SCRATCH = {
    "xb": ("sbuf", [128, 4 * TOTAL], "bfloat16"),
    "wb": ("sbuf", [128, 4 * KT * WM], "bfloat16"),
    "qx": ("sbuf", [128, TOTAL], "float8_e4m3fn_x4"),
    "sx": ("sbuf", [128, TOTAL], "uint8"),
    "qw": ("sbuf", [128, KT * WM], "float8_e4m3fn_x4"),
    "sw": ("sbuf", [128, KT * WM], "uint8"),
    "rx": ("sbuf", [128, TOTAL], "float8_e4m3fn_x4"),
    "rs": ("sbuf", [128, TOTAL], "uint8"),
    "ps": ("psum", [128, 512 * len(GROUPS)], "float32"),
    "yb": ("sbuf", [128, NC], "float32"),
}
SEMAPHORES = (["ld%d" % i for i in range(len(PIECES))] + ["q%d" % i for i in range(len(PIECES))]
              + ["ar%d" % k for k in range(len(SENDS))]
              + [n + "%d" % j for j in range(len(GROUPS)) for n in ("mm", "cp", "st")]
              + ["ldw", "qw", "sent"])


def rank_program(g, core, T, topo):
    rank = T.rank_of(core)
    if rank is None:
        return
    sem = T.sem
    dst = T.cores[T.tables["FROM"].index(rank)]
    assert topo.may_write(core, dst)
    rid, pid, _ = topo.addr(dst)
    mask = topo.mask(core, dst)
    ne = bin(mask).count("1")

    lq = [g.sync, g.scalar]
    for i, (a, b) in enumerate(PIECES):
        lq[i % 2].dma_start(T.xb[:, 4 * a:4 * b], T.x[:, 4 * a:4 * b]).then_inc(sem["ld%d" % i], 16)
    lq[len(PIECES) % 2].dma_start(T.wb[:], T.w[:]).then_inc(sem.ldw, 16)

    for i, (a, b) in enumerate(PIECES):
        g.vector.wait_ge(sem["ld%d" % i], 16)
        g.vector.quantize_mx(T.qx[:, a:b], T.sx[:, a:b], T.xb[:, 4 * a:4 * b]).then_inc(sem["q%d" % i], 1)
    g.vector.wait_ge(sem.ldw, 16)
    g.vector.quantize_mx(T.qw[:], T.sw[:], T.wb[:]).then_inc(sem.qw, 1)

    seen = set()
    for k, (kind, a, b) in enumerate(SENDS):
        for i, (pa, pb) in enumerate(PIECES):
            if pa < b and a < pb and i not in seen:
                g.wait_ge(sem["q%d" % i], 1)
                seen.add(i)
        if kind == "codes":
            src, out = T.qx[:, a:b].bitcast(dt.uint8), T.rx[:, a:b].bitcast(dt.uint8)
        else:
            src, out = T.sx[:, a:b], T.rs[:, a:b]
        g.remote_dma(out_ap=out, in_ap=src, remote_sem=sem["ar%d" % k], local_sem=sem.sent,
                     pid=pid, routing_id=rid, dma_engine_mask=mask)
    g.wait_ge(sem.sent, ne * len(SENDS))

    g.tensor.wait_ge(sem.qw, 1)
    got = set()
    for t in range(KT):
        for j, (a, b) in enumerate(GROUPS):
            lo, hi = NC * t + a, NC * t + b
            for k, (kind, sa, sb) in enumerate(SENDS):
                if sa < hi and lo < sb and k not in got:
                    g.tensor.wait_ge(sem["ar%d" % k], ne)
                    got.add(k)
            mm = g.tensor.matmul_mx(T.ps[:, 512 * j:512 * j + (b - a)],
                                    T.qw[:, WM * t:WM * (t + 1)], T.sw[:, WM * t:WM * (t + 1)],
                                    T.rx[:, lo:hi], T.rs[:, lo:hi], t == 0, t == KT - 1)
            if t == KT - 1:
                mm.then_inc(sem["mm%d" % j], 1)

    last = len(GROUPS) - 1
    for j, (a, b) in enumerate(GROUPS):
        bank = T.ps[:, 512 * j:512 * j + (b - a)]
        if j == last:
            g.vector.wait_ge(sem["mm%d" % j], 1)
            g.vector.tensor_copy(T.yb[:, a:b], bank).then_inc(sem["cp%d" % j], 1)
            q = g.sync
        else:
            g.scalar.wait_ge(sem["mm%d" % j], 1)
            g.scalar.activation(T.yb[:, a:b], bank, ActivationFunctionType.Copy).then_inc(sem["cp%d" % j], 1)
            q = g.scalar
        q.wait_ge(sem["cp%d" % j], 1)
        q.dma_start(T.y[:, a:b], T.yb[:, a:b]).then_inc(sem["st%d" % j], 16)
        q.wait_ge(sem["st%d" % j], 16)
